import numpy as np
import ml_dtypes


def mxq(x, axis, fmt="e4m3"):
    dtype, down = {"e4m3": (ml_dtypes.float8_e4m3fn, 7), "e5m2": (ml_dtypes.float8_e5m2, 14)}[fmt]
    v = np.moveaxis(np.asarray(x, np.float32).astype(ml_dtypes.bfloat16).astype(np.float64), axis, -1)
    blocks = v.reshape(v.shape[:-1] + (-1, 32))
    amax = np.abs(blocks).max(-1, keepdims=True)
    byte = np.maximum(np.where(amax > 0, np.frexp(amax)[1] - 1 + 127, 0) - down, 1)
    scale = np.exp2(byte - 127.0)
    codes = (blocks / scale).astype(np.float32).astype(dtype).astype(np.float64)
    return np.moveaxis((codes * scale).reshape(v.shape), -1, axis)


WIDE = False


def mx_kscale(k):
    if not WIDE:
        return np.ones(k)
    levels = np.array([10, -10, 5, -5, 0])
    if k % 512:
        return np.exp2(np.random.permutation(np.resize(levels, k // 32))).repeat(32)
    a = np.empty((k // 512, 16))
    for p in range(k // 512):
        a[p, :8] = np.random.permutation(np.resize(levels, 8))
        for g in range(8):
            far = levels[np.abs(levels - a[p, g]) >= 10]
            a[p, g + 8] = far[np.random.randint(len(far))]
    return np.exp2(a.ravel()).repeat(32)


def f64(x):
    return np.asarray(x).astype(np.float64)


def striped(idx):
    return np.tile(np.asarray(idx).reshape(-1, 16).T, (8, 1)).astype(np.uint16)


def unstriped(offs):
    return offs[:16].T.reshape(-1).astype(np.int64)


E2M1 = np.array([0.0, 0.5, 1.0, 1.5, 2.0, 3.0, 4.0, 6.0, -0.0, -0.5, -1.0, -1.5, -2.0, -3.0, -4.0, -6.0])


def pack_weight(w, fmt):
    k, n = w.shape
    w = f64(np.asarray(w, np.float32).astype(ml_dtypes.bfloat16)).reshape(k // 32, 32, n)
    amax = np.abs(w).max(1)
    if fmt == "e4m3":
        byte = np.frexp(amax)[1] - 1 + 127 - 7
    else:
        mant, ex = np.frexp(amax / 6.0)
        byte = np.where(mant > 0.5, ex, ex - 1) + 127
    byte = np.clip(np.where(amax > 0, byte, 1), 1, 254)
    scaled = (w * np.exp2(127.0 - byte)[:, None, :]).reshape(k, n).astype(np.float32)
    by_word = np.ascontiguousarray(scaled.reshape(k // 512, 128, 4, n).transpose(0, 1, 3, 2))
    if fmt == "e4m3":
        words = by_word.astype(ml_dtypes.float8_e4m3fn).view(np.uint8)
    else:
        c = by_word.astype(ml_dtypes.float4_e2m1fn).view(np.uint8) & 0xF
        words = (c[..., 0::2] | (c[..., 1::2] << 4)).reshape(k // 512, 128, 2 * n)
    return np.ascontiguousarray(words), np.ascontiguousarray(byte.astype(np.uint8).reshape(k // 512, 16, n))


def unpack_weight(words, scales, fmt):
    g, _, n = scales.shape
    words = np.ascontiguousarray(words).reshape(g, 128, n, -1)
    if fmt == "e4m3":
        vals = words.view(ml_dtypes.float8_e4m3fn).astype(np.float64)
    else:
        nib = np.empty((g, 128, n, 4), np.uint8)
        nib[..., 0::2] = words & 0xF
        nib[..., 1::2] = words >> 4
        vals = E2M1[nib]
    vals = vals * np.repeat(np.exp2(scales.astype(np.float64) - 127.0), 8, axis=1)[..., None]
    return vals.transpose(0, 1, 3, 2).reshape(g * 512, n)


D, E, T, I, Q = 512, 512, 2048, 512, 128


def setup_inputs():
    n = np.random.standard_normal
    idx = np.random.permutation(T)[:I]
    fd = mx_kscale(D)
    fi = mx_kscale(I)
    ti = np.ones(T)
    ti[idx] = fi
    keysp = pack_weight(n((D, T)) / fd[:, None], "e4m3")
    return {
        "query": (n((D, Q)) * 1.0 / np.sqrt(D) * fd[:, None]).astype(np.float32),
        "keys_words": keysp[0],
        "keys_scales": keysp[1],
        "floor": (np.random.uniform(0.05, 0.3, (Q, 1))).astype(np.float32),
        "reserve": (np.random.uniform(20.0, 100.0, (Q, 1))).astype(np.float32),
        "dquery": (n((D, Q)) * 0.6 / np.sqrt(D) * fd[:, None]).astype(np.float32),
        "os": (np.random.uniform(4.0, 16.0, (1, I)) * fi).astype(np.float32),
        "vals": (n((E, T)) / ti).astype(np.float32),
        "offs": striped(idx),
    }


def reference(query, keys_words, keys_scales, floor, reserve, dquery, os, vals, offs):
    idx = unstriped(offs)
    keysu = unpack_weight(keys_words, keys_scales, "e4m3")
    queryq = mxq(f64(query), 0, "e4m3")
    keysidxg = keysu[:, idx]
    a = queryq.T @ keysidxg
    dqueryq = mxq(f64(dquery), 0, "e4m3")
    ta = dqueryq.T @ keysidxg
    p = np.square(a) + f64(floor)
    z = np.sum(p, axis=1, keepdims=True) + f64(reserve)
    tp = ta * a * 2.0
    tz = np.sum(tp, axis=1, keepdims=True)
    tw = (tp - tz * p / z) / z
    wo1 = tw * f64(os)
    wt1 = wo1.T
    vt1 = f64(vals)[:, idx].T
    wt1q = mxq(wt1, 0, "e4m3")
    vt1q = mxq(vt1, 0, "e4m3")
    o = wt1q.T @ vt1q
    return o

@@ -1,0 +1,168 @@
+from contextlib import ExitStack
+
+import concourse.mybir as mybir
+from concourse.masks import make_identity
+
+D, E, T, SLOTS, Q = 512, 512, 2048, 512, 128
+FLOPS = 2 * Q * SLOTS * (2 * D + E)
+
+F32 = mybir.dt.float32
+BF16 = mybir.dt.bfloat16
+I32 = mybir.dt.int32
+U32 = mybir.dt.uint32
+U16 = mybir.dt.uint16
+U8 = mybir.dt.uint8
+FP8X4 = mybir.dt.float8_e4m3fn_x4
+ACT = mybir.ActivationFunctionType
+MULT = mybir.AluOpType.mult
+ADD = mybir.AluOpType.add
+
+P = 128
+PACK = 4
+E_BLOCKS = E // P
+
+
+def tile_attend_ttsquareshares_kernel(
+    tc, query, keys_words, keys_scales, row_floor, reserve, dquery, slot_factor, vals, offs, out
+):
+    nc = tc.nc
+    with ExitStack() as ctx:
+        sb = ctx.enter_context(tc.tile_pool(name="sb", bufs=1))
+        ps = ctx.enter_context(tc.psum_pool(name="ps", bufs=1))
+
+        offsets = sb.tile([P, SLOTS // 16], U16, name="offsets")
+        nc.sync.dma_start(offsets[:], offs)
+
+        pool_scales = sb.tile([P, T], U8, name="pool_scales", align_bytes=64)
+        nc.gpsimd.memset(pool_scales[:].bitcast(I32), 0)
+        for quad in range(4):
+            nc.gpsimd.dma_start(
+                out=pool_scales[32 * quad : 32 * quad + 4, :].bitcast(I32),
+                in_=keys_scales[0, 4 * quad : 4 * quad + 4, :].bitcast(I32),
+            )
+
+        pool_words = sb.tile([P, T], U32, name="pool_words", align_bytes=64)
+        nc.sync.dma_start(
+            out=pool_words[:].bitcast(I32),
+            in_=keys_words[0].rearrange("p n t -> p (n t)").bitcast(I32),
+        )
+
+        q_raw = [sb.tile([P, PACK, Q], F32, name="q_raw%d" % s) for s in range(2)]
+        for s, src in enumerate((query, dquery)):
+            nc.sync.dma_start(out=q_raw[s][:], in_=src.rearrange("(p t) q -> p t q", t=PACK))
+
+        floor_col = sb.tile([P, 1], F32, name="floor_col")
+        nc.sync.dma_start(out=floor_col[:], in_=row_floor)
+        reserve_col = sb.tile([P, 1], F32, name="reserve_col")
+        nc.sync.dma_start(out=reserve_col[:], in_=reserve)
+        factor = sb.tile([P, PACK], F32, name="factor")
+        nc.sync.dma_start(out=factor[:], in_=slot_factor.rearrange("o (p t) -> (o p) t", t=PACK))
+
+        pool_vals = [sb.tile([P, T], F32, name="pool_vals%d" % b) for b in range(E_BLOCKS)]
+        for b in range(E_BLOCKS):
+            nc.sync.dma_start(out=pool_vals[b][:], in_=vals[b * P : (b + 1) * P, :])
+
+        ident = sb.tile([P, P], F32, name="ident")
+        make_identity(nc, ident[:])
+        z_rest = sb.tile([P, 1], F32, name="z_rest")
+        nc.gpsimd.tensor_scalar(z_rest[:], floor_col[:], float(SLOTS), reserve_col[:], MULT, ADD)
+
+        q_bf = sb.tile([P, 2, Q, PACK], BF16, name="q_bf", align_bytes=64)
+        for s in range(2):
+            nc.scalar.copy(
+                out=q_bf[:, s].rearrange("p (c i) t -> p c t i", i=4),
+                in_=q_raw[s][:].rearrange("p t (c i) -> p c t i", i=4),
+            )
+        q_codes = sb.tile([P, 2 * Q], U32, name="q_codes", align_bytes=64)
+        q_scales = sb.tile([P, 2 * Q], U8, name="q_scales", align_bytes=64)
+        nc.vector.quantize_mx(
+            out=q_codes[:].bitcast(FP8X4),
+            scales=q_scales[:],
+            in_=q_bf[:].rearrange("p s q t -> p (s q t)"),
+        )
+
+        k_scales = sb.tile([P, SLOTS], U8, name="k_scales", align_bytes=64)
+        nc.vector.tensor_copy(k_scales[:], pool_scales[:].indirect(offsets[:]))
+        k_codes = sb.tile([P, SLOTS], U32, name="k_codes", align_bytes=64)
+        nc.vector.tensor_copy(k_codes[:], pool_words[:].indirect(offsets[:]))
+
+        scores = [ps.tile([P, SLOTS], F32, name="scores%d" % s) for s in range(2)]
+        for s in range(2):
+            cols = slice(s * Q, (s + 1) * Q)
+            nc.tensor.matmul_mx(
+                out=scores[s][:],
+                lhsT=q_codes[:, cols].bitcast(FP8X4),
+                lhsT_scale=q_scales[:, cols],
+                rhs=k_codes[:].bitcast(FP8X4),
+                rhs_scale=k_scales[:],
+                start=True,
+                stop=True,
+            )
+        a_dealt, ta_dealt = (s[:].rearrange("q (p t) -> q t p", t=PACK) for s in scores)
+
+        sq = sb.tile([P, PACK, P], F32, name="sq")
+        sq_sum = sb.tile([P, 1], F32, name="sq_sum")
+        nc.scalar.activation(sq[:], a_dealt, ACT.Square, accum_out=sq_sum[:])
+        ta2 = sb.tile([P, PACK, P], F32, name="ta2")
+        nc.scalar.activation(ta2[:], ta_dealt, ACT.Copy, scale=2.0)
+        part = sb.tile([P, PACK, P], F32, name="part")
+        nc.scalar.activation(part[:], sq[:], ACT.Identity, bias=floor_col[:])
+
+        z = sb.tile([P, 1], F32, name="z")
+        nc.vector.tensor_tensor(z[:], sq_sum[:], z_rest[:], ADD)
+        inv_z = sb.tile([P, 1], F32, name="inv_z")
+        nc.vector.reciprocal(inv_z[:], z[:])
+        tp_z = sb.tile([P, PACK, P], F32, name="tp_z")
+        tz_z = sb.tile([P, 1], F32, name="tz_z")
+        nc.vector.scalar_tensor_tensor(tp_z[:], a_dealt, inv_z[:], ta2[:], MULT, MULT, accum_out=tz_z[:])
+        slope = sb.tile([P, 1], F32, name="slope")
+        nc.vector.tensor_scalar(slope[:], tz_z[:], inv_z[:], -1.0, MULT, MULT)
+        tw = sb.tile([P, PACK, P], F32, name="tw")
+        nc.vector.scalar_tensor_tensor(tw[:], part[:], slope[:], tp_z[:], MULT, ADD)
+
+        tw_turned = ps.tile([P, PACK, Q], F32, name="tw_turned")
+        for t in range(PACK):
+            nc.tensor.transpose(tw_turned[:, t, :], tw[:, t, :], ident[:])
+        w_bf = sb.tile([P, Q, PACK], BF16, name="w_bf", align_bytes=64)
+        nc.vector.tensor_tensor(
+            w_bf[:],
+            tw_turned[:].rearrange("p t q -> p q t"),
+            factor[:].unsqueeze(1).to_broadcast([P, Q, PACK]),
+            MULT,
+        )
+        w_codes = sb.tile([P, Q], U32, name="w_codes", align_bytes=64)
+        w_scales = sb.tile([P, Q], U8, name="w_scales", align_bytes=64)
+        nc.vector.quantize_mx(
+            out=w_codes[:].bitcast(FP8X4),
+            scales=w_scales[:],
+            in_=w_bf[:].rearrange("p q t -> p (q t)"),
+        )
+
+        for b in range(E_BLOCKS):
+            v_listed = sb.tile([P, SLOTS], BF16, name="v_listed%d" % b, align_bytes=64)
+            nc.vector.tensor_copy(v_listed[:], pool_vals[b][:].indirect(offsets[:]))
+            pairs = v_listed[:].bitcast(F32)
+            v_turned = ps.tile([P, 2, P], F32, name="v_turned", bufs=2)
+            for u in range(2):
+                nc.tensor.transpose(v_turned[:, u, :], pairs[:, u :: 2], ident[:])
+            v_bf = sb.tile([P, P * PACK], BF16, name="v_bf%d" % b, align_bytes=64)
+            nc.scalar.copy(
+                out=v_bf[:].bitcast(F32).rearrange("p (e u) -> p e u", u=2),
+                in_=v_turned[:].rearrange("p u e -> p e u"),
+            )
+            v_codes = sb.tile([P, P], U32, name="v_codes%d" % b, align_bytes=64)
+            v_scales = sb.tile([P, P], U8, name="v_scales%d" % b, align_bytes=64)
+            nc.vector.quantize_mx(out=v_codes[:].bitcast(FP8X4), scales=v_scales[:], in_=v_bf[:])
+            acc = ps.tile([P, P], F32, name="acc", bufs=3)
+            nc.tensor.matmul_mx(
+                out=acc[:],
+                lhsT=w_codes[:].bitcast(FP8X4),
+                lhsT_scale=w_scales[:],
+                rhs=v_codes[:].bitcast(FP8X4),
+                rhs_scale=v_scales[:],
+                start=True,
+                stop=True,
+            )
+            result = sb.tile([P, P], F32, name="result%d" % b)
+            nc.scalar.copy(out=result[:], in_=acc[:])
+            nc.sync.dma_start(out=out[:, b * P : (b + 1) * P], in_=result[:])

@@ -1,7 +1,6 @@
 from contextlib import ExitStack
 
 import concourse.mybir as mybir
-from concourse.masks import make_identity
 
 D, E, T, SLOTS, Q = 512, 512, 2048, 512, 128
 FLOPS = 2 * Q * SLOTS * (2 * D + E)
@@ -15,11 +14,14 @@ U8 = mybir.dt.uint8
 FP8X4 = mybir.dt.float8_e4m3fn_x4
 ACT = mybir.ActivationFunctionType
 MULT = mybir.AluOpType.mult
-ADD = mybir.AluOpType.add
+SUB = mybir.AluOpType.subtract
 
 P = 128
 PACK = 4
+QUADRANT = 32
 E_BLOCKS = E // P
+LAST = E_BLOCKS - 1
+E_RANGES = ((0, 2 * P), (2 * P, LAST * P), (LAST * P, E))
 
 
 def tile_attend_ttsquareshares_kernel(
@@ -32,40 +34,53 @@ def tile_attend_ttsquareshares_kernel(
 
         offsets = sb.tile([P, SLOTS // 16], U16, name="offsets")
         nc.sync.dma_start(offsets[:], offs)
-
-        pool_scales = sb.tile([P, T], U8, name="pool_scales", align_bytes=64)
-        nc.gpsimd.memset(pool_scales[:].bitcast(I32), 0)
-        for quad in range(4):
-            nc.gpsimd.dma_start(
-                out=pool_scales[32 * quad : 32 * quad + 4, :].bitcast(I32),
-                in_=keys_scales[0, 4 * quad : 4 * quad + 4, :].bitcast(I32),
-            )
-
         pool_words = sb.tile([P, T], U32, name="pool_words", align_bytes=64)
         nc.sync.dma_start(
             out=pool_words[:].bitcast(I32),
             in_=keys_words[0].rearrange("p n t -> p (n t)").bitcast(I32),
         )
-
         q_raw = [sb.tile([P, PACK, Q], F32, name="q_raw%d" % s) for s in range(2)]
         for s, src in enumerate((query, dquery)):
             nc.sync.dma_start(out=q_raw[s][:], in_=src.rearrange("(p t) q -> p t q", t=PACK))
-
-        floor_col = sb.tile([P, 1], F32, name="floor_col")
-        nc.sync.dma_start(out=floor_col[:], in_=row_floor)
-        reserve_col = sb.tile([P, 1], F32, name="reserve_col")
-        nc.sync.dma_start(out=reserve_col[:], in_=reserve)
-        factor = sb.tile([P, PACK], F32, name="factor")
-        nc.sync.dma_start(out=factor[:], in_=slot_factor.rearrange("o (p t) -> (o p) t", t=PACK))
-
-        pool_vals = [sb.tile([P, T], F32, name="pool_vals%d" % b) for b in range(E_BLOCKS)]
-        for b in range(E_BLOCKS):
-            nc.sync.dma_start(out=pool_vals[b][:], in_=vals[b * P : (b + 1) * P, :])
+        pool_scales = sb.tile([P, T], U8, name="pool_scales", align_bytes=64)
+        nc.gpsimd.memset(pool_scales[:].bitcast(I32), 0)
+        for r in range(PACK):
+            nc.sync.dma_start(
+                out=pool_scales[r:P:QUADRANT, :].bitcast(I32),
+                in_=keys_scales[0, r::PACK, :].bitcast(I32),
+            )
 
         ident = sb.tile([P, P], F32, name="ident")
-        make_identity(nc, ident[:])
-        z_rest = sb.tile([P, 1], F32, name="z_rest")
-        nc.gpsimd.tensor_scalar(z_rest[:], floor_col[:], float(SLOTS), reserve_col[:], MULT, ADD)
+        with tc.tile_pool(name="setup", bufs=1) as setup:
+            zeros = setup.tile([P, P], F32, name="zeros")
+            nc.gpsimd.memset(zeros[:], 0.0)
+            nc.gpsimd.affine_select(
+                out=ident[:],
+                in_=zeros[:],
+                pattern=[[-1, P]],
+                compare_op=mybir.AluOpType.not_equal,
+                fill=1.0,
+                base=0,
+                channel_multiplier=1,
+            )
+        late = ctx.enter_context(tc.tile_pool(name="late", bufs=1))
+
+        pool_vals = [
+            late.tile([P, T], F32, name="pool_vals%d" % b, tag="vals%d" % b, align_bytes=64)
+            for b in range(E_BLOCKS)
+        ]
+        factor = late.tile([P, PACK], F32, name="factor")
+        floor_col = late.tile([P, 1], F32, name="floor_col")
+        reserve_col = late.tile([P, 1], F32, name="reserve_col")
+        nc.sync.dma_start(out=pool_vals[0][:], in_=vals[:P, :])
+        nc.sync.dma_start(out=floor_col[:], in_=row_floor)
+        nc.sync.dma_start(out=reserve_col[:], in_=reserve)
+        nc.sync.dma_start(out=factor[:], in_=slot_factor.rearrange("o (p t) -> (o p) t", t=PACK))
+        for b in range(1, E_BLOCKS):
+            nc.sync.dma_start(out=pool_vals[b][:], in_=vals[b * P : (b + 1) * P, :])
+
+        neg_z_rest = sb.tile([P, 1], F32, name="neg_z_rest")
+        nc.gpsimd.tensor_scalar(neg_z_rest[:], floor_col[:], -float(SLOTS), reserve_col[:], MULT, SUB)
 
         q_bf = sb.tile([P, 2, Q, PACK], BF16, name="q_bf", align_bytes=64)
         for s in range(2):
@@ -86,83 +101,110 @@ def tile_attend_ttsquareshares_kernel(
         k_codes = sb.tile([P, SLOTS], U32, name="k_codes", align_bytes=64)
         nc.vector.tensor_copy(k_codes[:], pool_words[:].indirect(offsets[:]))
 
-        scores = [ps.tile([P, SLOTS], F32, name="scores%d" % s) for s in range(2)]
+        scores = [ps.tile([P, SLOTS], F32, name="scores%d" % s, tag="scores%d" % s) for s in range(2)]
         for s in range(2):
-            cols = slice(s * Q, (s + 1) * Q)
+            rows = slice(s * Q, (s + 1) * Q)
             nc.tensor.matmul_mx(
                 out=scores[s][:],
-                lhsT=q_codes[:, cols].bitcast(FP8X4),
-                lhsT_scale=q_scales[:, cols],
+                lhsT=q_codes[:, rows].bitcast(FP8X4),
+                lhsT_scale=q_scales[:, rows],
                 rhs=k_codes[:].bitcast(FP8X4),
                 rhs_scale=k_scales[:],
                 start=True,
                 stop=True,
             )
-        a_dealt, ta_dealt = (s[:].rearrange("q (p t) -> q t p", t=PACK) for s in scores)
+        a_dealt, ta_dealt = (bank[:].rearrange("q (p t) -> q t p", t=PACK) for bank in scores)
 
         sq = sb.tile([P, PACK, P], F32, name="sq")
         sq_sum = sb.tile([P, 1], F32, name="sq_sum")
         nc.scalar.activation(sq[:], a_dealt, ACT.Square, accum_out=sq_sum[:])
-        ta2 = sb.tile([P, PACK, P], F32, name="ta2")
-        nc.scalar.activation(ta2[:], ta_dealt, ACT.Copy, scale=2.0)
-        part = sb.tile([P, PACK, P], F32, name="part")
-        nc.scalar.activation(part[:], sq[:], ACT.Identity, bias=floor_col[:])
-
-        z = sb.tile([P, 1], F32, name="z")
-        nc.vector.tensor_tensor(z[:], sq_sum[:], z_rest[:], ADD)
-        inv_z = sb.tile([P, 1], F32, name="inv_z")
-        nc.vector.reciprocal(inv_z[:], z[:])
+        neg_z = sb.tile([P, 1], F32, name="neg_z")
+        nc.scalar.activation(neg_z[:], sq_sum[:], ACT.Identity, scale=-1.0, bias=neg_z_rest[:])
+        neg_ta2 = sb.tile([P, PACK, P], F32, name="neg_ta2")
+        nc.scalar.activation(neg_ta2[:], ta_dealt, ACT.Copy, scale=-2.0)
+        neg_inv_z = sb.tile([P, 1], F32, name="neg_inv_z")
+        nc.vector.reciprocal(neg_inv_z[:], neg_z[:])
+        neg_floor_z = sb.tile([P, 1], F32, name="neg_floor_z")
+        nc.vector.tensor_tensor(neg_floor_z[:], floor_col[:], neg_inv_z[:], MULT)
+        neg_share = sb.tile([P, PACK, P], F32, name="neg_share")
+        nc.scalar.activation(neg_share[:], sq[:], ACT.Identity, scale=neg_inv_z[:], bias=neg_floor_z[:])
         tp_z = sb.tile([P, PACK, P], F32, name="tp_z")
         tz_z = sb.tile([P, 1], F32, name="tz_z")
-        nc.vector.scalar_tensor_tensor(tp_z[:], a_dealt, inv_z[:], ta2[:], MULT, MULT, accum_out=tz_z[:])
-        slope = sb.tile([P, 1], F32, name="slope")
-        nc.vector.tensor_scalar(slope[:], tz_z[:], inv_z[:], -1.0, MULT, MULT)
-        tw = sb.tile([P, PACK, P], F32, name="tw")
-        nc.vector.scalar_tensor_tensor(tw[:], part[:], slope[:], tp_z[:], MULT, ADD)
+        nc.vector.scalar_tensor_tensor(tp_z[:], a_dealt, neg_inv_z[:], neg_ta2[:], MULT, MULT, accum_out=tz_z[:])
+        pull = sb.tile([P, PACK, P], F32, name="pull")
+        nc.scalar.activation(pull[:], neg_share[:], ACT.Copy, scale=tz_z[:])
 
-        tw_turned = ps.tile([P, PACK, Q], F32, name="tw_turned")
-        for t in range(PACK):
-            nc.tensor.transpose(tw_turned[:, t, :], tw[:, t, :], ident[:])
-        w_bf = sb.tile([P, Q, PACK], BF16, name="w_bf", align_bytes=64)
+        tw_turned = ps.tile([P, PACK, Q], F32, name="tw_turned", tag="tw")
+        for n, term in enumerate((tp_z, pull)):
+            for t in range(PACK):
+                nc.tensor.matmul(
+                    tw_turned[:, t, :],
+                    lhsT=term[:, t, :],
+                    rhs=ident[:],
+                    is_transpose=True,
+                    start=(n == 0 and t == 0),
+                    stop=(n == 1 and t == PACK - 1),
+                )
+
+        listed = []
+        for b in range(E_BLOCKS):
+            v_listed = sb.tile([P, SLOTS], BF16, name="v_listed%d" % b, align_bytes=64)
+            nc.vector.tensor_copy(v_listed[:], pool_vals[b][:].indirect(offsets[:]))
+            listed.append(v_listed)
+
+        w_bf = late.tile([P, Q, PACK], BF16, name="w_bf", tag="vals%d" % (LAST - 1), align_bytes=64)
         nc.vector.tensor_tensor(
             w_bf[:],
             tw_turned[:].rearrange("p t q -> p q t"),
             factor[:].unsqueeze(1).to_broadcast([P, Q, PACK]),
             MULT,
         )
-        w_codes = sb.tile([P, Q], U32, name="w_codes", align_bytes=64)
+
+        v_bf = sb.tile([P, E * PACK], BF16, name="v_bf", align_bytes=64)
+        v_pairs = v_bf[:].bitcast(F32)
+        for b in range(E_BLOCKS):
+            listed_pairs = listed[b][:].bitcast(F32)
+            bank_tag = "tw" if b == 1 else "turned%d" % b
+            v_turned = ps.tile([P, 2, P], F32, name="v_turned%d" % b, tag=bank_tag)
+            for u in range(2):
+                nc.tensor.transpose(v_turned[:, u, :], listed_pairs[:, u::2], ident[:])
+            nc.scalar.copy(
+                out=v_pairs[:, b * 2 * P : (b + 1) * 2 * P].rearrange("p (e u) -> p e u", u=2),
+                in_=v_turned[:].rearrange("p u e -> p e u"),
+            )
+
+        held_codes = late.tile([P, Q + LAST * P], U32, name="held_codes", tag="vals%d" % LAST, align_bytes=64)
+        last_codes = sb.tile([P, P], U32, name="last_codes", align_bytes=64)
+        w_codes = held_codes[:, :Q]
         w_scales = sb.tile([P, Q], U8, name="w_scales", align_bytes=64)
         nc.vector.quantize_mx(
-            out=w_codes[:].bitcast(FP8X4),
+            out=w_codes.bitcast(FP8X4),
             scales=w_scales[:],
             in_=w_bf[:].rearrange("p q t -> p (q t)"),
         )
 
-        for b in range(E_BLOCKS):
-            v_listed = sb.tile([P, SLOTS], BF16, name="v_listed%d" % b, align_bytes=64)
-            nc.vector.tensor_copy(v_listed[:], pool_vals[b][:].indirect(offsets[:]))
-            pairs = v_listed[:].bitcast(F32)
-            v_turned = ps.tile([P, 2, P], F32, name="v_turned", bufs=2)
-            for u in range(2):
-                nc.tensor.transpose(v_turned[:, u, :], pairs[:, u :: 2], ident[:])
-            v_bf = sb.tile([P, P * PACK], BF16, name="v_bf%d" % b, align_bytes=64)
-            nc.scalar.copy(
-                out=v_bf[:].bitcast(F32).rearrange("p (e u) -> p e u", u=2),
-                in_=v_turned[:].rearrange("p u e -> p e u"),
+        for g, (lo, hi) in enumerate(E_RANGES):
+            is_last = hi == E
+            v_codes = last_codes[:] if is_last else held_codes[:, Q + lo : Q + hi]
+            v_scales = sb.tile([P, hi - lo], U8, name="v_scales%d" % g, align_bytes=64)
+            nc.vector.quantize_mx(
+                out=v_codes.bitcast(FP8X4),
+                scales=v_scales[:],
+                in_=v_bf[:, lo * PACK : hi * PACK],
             )
-            v_codes = sb.tile([P, P], U32, name="v_codes%d" % b, align_bytes=64)
-            v_scales = sb.tile([P, P], U8, name="v_scales%d" % b, align_bytes=64)
-            nc.vector.quantize_mx(out=v_codes[:].bitcast(FP8X4), scales=v_scales[:], in_=v_bf[:])
-            acc = ps.tile([P, P], F32, name="acc", bufs=3)
+            acc = ps.tile([P, hi - lo], F32, name="acc%d" % g, tag="acc_last" if is_last else "scores%d" % g)
             nc.tensor.matmul_mx(
                 out=acc[:],
-                lhsT=w_codes[:].bitcast(FP8X4),
+                lhsT=w_codes.bitcast(FP8X4),
                 lhsT_scale=w_scales[:],
-                rhs=v_codes[:].bitcast(FP8X4),
+                rhs=v_codes.bitcast(FP8X4),
                 rhs_scale=v_scales[:],
                 start=True,
                 stop=True,
             )
-            result = sb.tile([P, P], F32, name="result%d" % b)
-            nc.scalar.copy(out=result[:], in_=acc[:])
-            nc.sync.dma_start(out=out[:, b * P : (b + 1) * P], in_=result[:])
+            result = sb.tile([P, hi - lo], F32, name="result%d" % g)
+            if is_last:
+                nc.vector.tensor_copy(out=result[:], in_=acc[:])
+            else:
+                nc.scalar.copy(out=result[:], in_=acc[:])
+            nc.sync.dma_start(out=out[:, lo:hi], in_=result[:])

from contextlib import ExitStack

import concourse.mybir as mybir

D, E, T, SLOTS, Q = 512, 512, 2048, 512, 128
FLOPS = 2 * Q * SLOTS * (2 * D + E)

F32 = mybir.dt.float32
BF16 = mybir.dt.bfloat16
I32 = mybir.dt.int32
U32 = mybir.dt.uint32
U16 = mybir.dt.uint16
U8 = mybir.dt.uint8
FP8X4 = mybir.dt.float8_e4m3fn_x4
ACT = mybir.ActivationFunctionType
MULT = mybir.AluOpType.mult
SUB = mybir.AluOpType.subtract

P = 128
PACK = 4
QUADRANT = 32
E_BLOCKS = E // P
LAST = E_BLOCKS - 1
E_RANGES = ((0, 2 * P), (2 * P, LAST * P), (LAST * P, E))


def tile_attend_ttsquareshares_kernel(
    tc, query, keys_words, keys_scales, row_floor, reserve, dquery, slot_factor, vals, offs, out
):
    nc = tc.nc
    with ExitStack() as ctx:
        sb = ctx.enter_context(tc.tile_pool(name="sb", bufs=1))
        ps = ctx.enter_context(tc.psum_pool(name="ps", bufs=1))

        offsets = sb.tile([P, SLOTS // 16], U16, name="offsets")
        nc.sync.dma_start(offsets[:], offs)
        pool_words = sb.tile([P, T], U32, name="pool_words", align_bytes=64)
        nc.sync.dma_start(
            out=pool_words[:].bitcast(I32),
            in_=keys_words[0].rearrange("p n t -> p (n t)").bitcast(I32),
        )
        q_raw = [sb.tile([P, PACK, Q], F32, name="q_raw%d" % s) for s in range(2)]
        for s, src in enumerate((query, dquery)):
            nc.sync.dma_start(out=q_raw[s][:], in_=src.rearrange("(p t) q -> p t q", t=PACK))
        pool_scales = sb.tile([P, T], U8, name="pool_scales", align_bytes=64)
        nc.gpsimd.memset(pool_scales[:].bitcast(I32), 0)
        for r in range(PACK):
            nc.sync.dma_start(
                out=pool_scales[r:P:QUADRANT, :].bitcast(I32),
                in_=keys_scales[0, r::PACK, :].bitcast(I32),
            )

        ident = sb.tile([P, P], F32, name="ident")
        with tc.tile_pool(name="setup", bufs=1) as setup:
            zeros = setup.tile([P, P], F32, name="zeros")
            nc.gpsimd.memset(zeros[:], 0.0)
            nc.gpsimd.affine_select(
                out=ident[:],
                in_=zeros[:],
                pattern=[[-1, P]],
                compare_op=mybir.AluOpType.not_equal,
                fill=1.0,
                base=0,
                channel_multiplier=1,
            )
        late = ctx.enter_context(tc.tile_pool(name="late", bufs=1))

        pool_vals = [
            late.tile([P, T], F32, name="pool_vals%d" % b, tag="vals%d" % b, align_bytes=64)
            for b in range(E_BLOCKS)
        ]
        factor = late.tile([P, PACK], F32, name="factor")
        floor_col = late.tile([P, 1], F32, name="floor_col")
        reserve_col = late.tile([P, 1], F32, name="reserve_col")
        nc.sync.dma_start(out=pool_vals[0][:], in_=vals[:P, :])
        nc.sync.dma_start(out=floor_col[:], in_=row_floor)
        nc.sync.dma_start(out=reserve_col[:], in_=reserve)
        nc.sync.dma_start(out=factor[:], in_=slot_factor.rearrange("o (p t) -> (o p) t", t=PACK))
        for b in range(1, E_BLOCKS):
            nc.sync.dma_start(out=pool_vals[b][:], in_=vals[b * P : (b + 1) * P, :])

        neg_z_rest = sb.tile([P, 1], F32, name="neg_z_rest")
        nc.gpsimd.tensor_scalar(neg_z_rest[:], floor_col[:], -float(SLOTS), reserve_col[:], MULT, SUB)

        q_bf = sb.tile([P, 2, Q, PACK], BF16, name="q_bf", align_bytes=64)
        for s in range(2):
            nc.scalar.copy(
                out=q_bf[:, s].rearrange("p (c i) t -> p c t i", i=4),
                in_=q_raw[s][:].rearrange("p t (c i) -> p c t i", i=4),
            )
        q_codes = sb.tile([P, 2 * Q], U32, name="q_codes", align_bytes=64)
        q_scales = sb.tile([P, 2 * Q], U8, name="q_scales", align_bytes=64)
        nc.vector.quantize_mx(
            out=q_codes[:].bitcast(FP8X4),
            scales=q_scales[:],
            in_=q_bf[:].rearrange("p s q t -> p (s q t)"),
        )

        k_scales = sb.tile([P, SLOTS], U8, name="k_scales", align_bytes=64)
        nc.vector.tensor_copy(k_scales[:], pool_scales[:].indirect(offsets[:]))
        k_codes = sb.tile([P, SLOTS], U32, name="k_codes", align_bytes=64)
        nc.vector.tensor_copy(k_codes[:], pool_words[:].indirect(offsets[:]))

        scores = [ps.tile([P, SLOTS], F32, name="scores%d" % s, tag="scores%d" % s) for s in range(2)]
        for s in range(2):
            rows = slice(s * Q, (s + 1) * Q)
            nc.tensor.matmul_mx(
                out=scores[s][:],
                lhsT=q_codes[:, rows].bitcast(FP8X4),
                lhsT_scale=q_scales[:, rows],
                rhs=k_codes[:].bitcast(FP8X4),
                rhs_scale=k_scales[:],
                start=True,
                stop=True,
            )
        a_dealt, ta_dealt = (bank[:].rearrange("q (p t) -> q t p", t=PACK) for bank in scores)

        sq = sb.tile([P, PACK, P], F32, name="sq")
        sq_sum = sb.tile([P, 1], F32, name="sq_sum")
        nc.scalar.activation(sq[:], a_dealt, ACT.Square, accum_out=sq_sum[:])
        neg_z = sb.tile([P, 1], F32, name="neg_z")
        nc.scalar.activation(neg_z[:], sq_sum[:], ACT.Identity, scale=-1.0, bias=neg_z_rest[:])
        neg_ta2 = sb.tile([P, PACK, P], F32, name="neg_ta2")
        nc.scalar.activation(neg_ta2[:], ta_dealt, ACT.Copy, scale=-2.0)
        neg_inv_z = sb.tile([P, 1], F32, name="neg_inv_z")
        nc.vector.reciprocal(neg_inv_z[:], neg_z[:])
        neg_floor_z = sb.tile([P, 1], F32, name="neg_floor_z")
        nc.vector.tensor_tensor(neg_floor_z[:], floor_col[:], neg_inv_z[:], MULT)
        neg_share = sb.tile([P, PACK, P], F32, name="neg_share")
        nc.scalar.activation(neg_share[:], sq[:], ACT.Identity, scale=neg_inv_z[:], bias=neg_floor_z[:])
        tp_z = sb.tile([P, PACK, P], F32, name="tp_z")
        tz_z = sb.tile([P, 1], F32, name="tz_z")
        nc.vector.scalar_tensor_tensor(tp_z[:], a_dealt, neg_inv_z[:], neg_ta2[:], MULT, MULT, accum_out=tz_z[:])
        pull = sb.tile([P, PACK, P], F32, name="pull")
        nc.scalar.activation(pull[:], neg_share[:], ACT.Copy, scale=tz_z[:])

        tw_turned = ps.tile([P, PACK, Q], F32, name="tw_turned", tag="tw")
        for n, term in enumerate((tp_z, pull)):
            for t in range(PACK):
                nc.tensor.matmul(
                    tw_turned[:, t, :],
                    lhsT=term[:, t, :],
                    rhs=ident[:],
                    is_transpose=True,
                    start=(n == 0 and t == 0),
                    stop=(n == 1 and t == PACK - 1),
                )

        listed = []
        for b in range(E_BLOCKS):
            v_listed = sb.tile([P, SLOTS], BF16, name="v_listed%d" % b, align_bytes=64)
            nc.vector.tensor_copy(v_listed[:], pool_vals[b][:].indirect(offsets[:]))
            listed.append(v_listed)

        w_bf = late.tile([P, Q, PACK], BF16, name="w_bf", tag="vals%d" % (LAST - 1), align_bytes=64)
        nc.vector.tensor_tensor(
            w_bf[:],
            tw_turned[:].rearrange("p t q -> p q t"),
            factor[:].unsqueeze(1).to_broadcast([P, Q, PACK]),
            MULT,
        )

        v_bf = sb.tile([P, E * PACK], BF16, name="v_bf", align_bytes=64)
        v_pairs = v_bf[:].bitcast(F32)
        for b in range(E_BLOCKS):
            listed_pairs = listed[b][:].bitcast(F32)
            bank_tag = "tw" if b == 1 else "turned%d" % b
            v_turned = ps.tile([P, 2, P], F32, name="v_turned%d" % b, tag=bank_tag)
            for u in range(2):
                nc.tensor.transpose(v_turned[:, u, :], listed_pairs[:, u::2], ident[:])
            nc.scalar.copy(
                out=v_pairs[:, b * 2 * P : (b + 1) * 2 * P].rearrange("p (e u) -> p e u", u=2),
                in_=v_turned[:].rearrange("p u e -> p e u"),
            )

        held_codes = late.tile([P, Q + LAST * P], U32, name="held_codes", tag="vals%d" % LAST, align_bytes=64)
        last_codes = sb.tile([P, P], U32, name="last_codes", align_bytes=64)
        w_codes = held_codes[:, :Q]
        w_scales = sb.tile([P, Q], U8, name="w_scales", align_bytes=64)
        nc.vector.quantize_mx(
            out=w_codes.bitcast(FP8X4),
            scales=w_scales[:],
            in_=w_bf[:].rearrange("p q t -> p (q t)"),
        )

        for g, (lo, hi) in enumerate(E_RANGES):
            is_last = hi == E
            v_codes = last_codes[:] if is_last else held_codes[:, Q + lo : Q + hi]
            v_scales = sb.tile([P, hi - lo], U8, name="v_scales%d" % g, align_bytes=64)
            nc.vector.quantize_mx(
                out=v_codes.bitcast(FP8X4),
                scales=v_scales[:],
                in_=v_bf[:, lo * PACK : hi * PACK],
            )
            acc = ps.tile([P, hi - lo], F32, name="acc%d" % g, tag="acc_last" if is_last else "scores%d" % g)
            nc.tensor.matmul_mx(
                out=acc[:],
                lhsT=w_codes.bitcast(FP8X4),
                lhsT_scale=w_scales[:],
                rhs=v_codes.bitcast(FP8X4),
                rhs_scale=v_scales[:],
                start=True,
                stop=True,
            )
            result = sb.tile([P, hi - lo], F32, name="result%d" % g)
            if is_last:
                nc.vector.tensor_copy(out=result[:], in_=acc[:])
            else:
                nc.scalar.copy(out=result[:], in_=acc[:])
            nc.sync.dma_start(out=out[:, lo:hi], in_=result[:])
